import numpy as np
import ml_dtypes

BF16 = ml_dtypes.bfloat16


def bf(x):
    return np.asarray(x, np.float32).astype(BF16)


def f32(x):
    return np.asarray(x, np.float32)


def f64(x):
    return np.asarray(x).astype(np.float64)


def striped(idx):
    return np.concatenate([l.reshape(-1, 16).T for l in idx])


def rows(idx, k):
    return np.tile(np.repeat(idx, 16, axis=0), (k // (16 * 8), 1))


def look(tab, idx):
    return np.take_along_axis(f64(tab), rows(idx, len(tab)), axis=1)


K, S, V, N, M = 256, 2048, 1024, 1024, 128


def setup_inputs():
    return {"tab": f32(np.random.standard_normal((2, K, S))), "y": f32(1.0 * np.random.standard_normal((K, V))), "w": bf(np.random.standard_normal((K, M)) / np.sqrt(K)), "b": f32(0.5 * np.random.standard_normal((M, 1))), "offs": striped(np.stack([np.random.permutation(S)[:N] for _ in range(8)]))}


def reference(tab, y, w, b, offs):
    idx = np.stack([g.T.reshape(-1) for g in np.split(offs, 8)])
    x = look(tab[0], idx) / (1.0 + np.exp(-look(tab[0], idx))) * f64(y) + look(tab[1], idx)
    return np.maximum(f64(w).T @ x + f64(b), 0.0)

@@ -1,0 +1,73 @@
+import concourse.mybir as mybir
+
+F32, BF16, U16 = mybir.dt.float32, mybir.dt.bfloat16, mybir.dt.uint16
+MULT, ADD = mybir.AluOpType.mult, mybir.AluOpType.add
+SILU, RELU = mybir.ActivationFunctionType.Silu, mybir.ActivationFunctionType.Relu
+
+P = 128
+ROWS = 256
+PLACES = 2048
+N = 1024
+M = 128
+PIECE = 512
+
+FLOPS = 2 * ROWS * N * M
+
+
+def tile_lookup_resglu_relu_kernel(tc, tab, y, w, b, offs, out):
+    nc = tc.nc
+    n_blocks = ROWS // P
+    n_pieces = N // PIECE
+    list_columns = PIECE // 16
+
+    with (
+        tc.tile_pool(name="held", bufs=1) as held,
+        tc.tile_pool(name="work", bufs=n_blocks * n_pieces) as work,
+        tc.psum_pool(name="sums", bufs=1) as sums,
+    ):
+        offsets = held.tile([P, N // 16], U16, name="offsets")
+        nc.sync.dma_start(offsets[:], offs)
+        gates, shifts, streams = [], [], []
+        for k in range(n_blocks):
+            rows = slice(k * P, (k + 1) * P)
+            gate = held.tile([P, PLACES], F32, name=f"gate{k}")
+            nc.sync.dma_start(gate[:], tab[0, rows, :])
+            stream = held.tile([P, N], F32, name=f"stream{k}")
+            nc.sync.dma_start(stream[:], y[rows, :])
+            shift = held.tile([P, PLACES], F32, name=f"shift{k}")
+            nc.sync.dma_start(shift[:], tab[1, rows, :])
+            gates.append(gate)
+            streams.append(stream)
+            shifts.append(shift)
+
+        weights = held.tile([P, n_blocks, M], BF16, name="weights")
+        nc.scalar.dma_start(weights[:], w.rearrange("(k p) m -> p k m", p=P))
+        bias = held.tile([M, 1], F32, name="bias")
+        nc.scalar.dma_start(bias[:], b)
+
+        totals = [sums.tile([M, PIECE], F32, name=f"total{i}") for i in range(n_pieces)]
+        for k in range(n_blocks):
+            lists = [offsets[:, i * list_columns : (i + 1) * list_columns] for i in range(n_pieces)]
+            gated = []
+            for i in range(n_pieces):
+                part = work.tile([P, PIECE], F32, name="part", tag="part")
+                nc.scalar.activation(part[:], gates[k][:].indirect(lists[i]), SILU)
+                gated.append(part)
+            products = []
+            for i in range(n_pieces):
+                product = work.tile([P, PIECE], F32, name="product", tag="product")
+                nc.vector.tensor_tensor(product[:], gated[i][:], streams[k][:, i * PIECE : (i + 1) * PIECE], MULT)
+                products.append(product)
+            for i in range(n_pieces):
+                x = work.tile([P, PIECE], F32, name="x", tag="x")
+                nc.vector.tensor_tensor(x[:], shifts[k][:].indirect(lists[i]), products[i][:], ADD)
+                x_rounded = work.tile([P, PIECE], BF16, name="x_rounded", tag="x_rounded")
+                nc.scalar.copy(x_rounded[:], x[:])
+                nc.tensor.matmul(
+                    totals[i][:], weights[:, k, :], x_rounded[:], start=(k == 0), stop=(k == n_blocks - 1)
+                )
+
+        for i in range(n_pieces):
+            result = work.tile([M, PIECE], F32, name="result", tag="result")
+            nc.scalar.activation(result[:], totals[i][:], RELU, bias=bias[:, 0:1])
+            nc.sync.dma_start(out[:, i * PIECE : (i + 1) * PIECE], result[:])

@@ -1,7 +1,7 @@
 import concourse.mybir as mybir
 
 F32, BF16, U16 = mybir.dt.float32, mybir.dt.bfloat16, mybir.dt.uint16
-MULT, ADD = mybir.AluOpType.mult, mybir.AluOpType.add
+MULT, ADD, MAX = mybir.AluOpType.mult, mybir.AluOpType.add, mybir.AluOpType.max
 SILU, RELU = mybir.ActivationFunctionType.Silu, mybir.ActivationFunctionType.Relu
 
 P = 128
@@ -10,6 +10,7 @@ PLACES = 2048
 N = 1024
 M = 128
 PIECE = 512
+HALF = PIECE // 2
 
 FLOPS = 2 * ROWS * N * M
 
@@ -45,7 +46,7 @@ def tile_lookup_resglu_relu_kernel(tc, tab, y, w, b, offs, out):
         bias = held.tile([M, 1], F32, name="bias")
         nc.scalar.dma_start(bias[:], b)
 
-        totals = [sums.tile([M, PIECE], F32, name=f"total{i}") for i in range(n_pieces)]
+        totals = [sums.tile([M, HALF], F32, name=f"total{q}") for q in range(2 * n_pieces)]
         for k in range(n_blocks):
             lists = [offsets[:, i * list_columns : (i + 1) * list_columns] for i in range(n_pieces)]
             gated = []
@@ -62,12 +63,24 @@ def tile_lookup_resglu_relu_kernel(tc, tab, y, w, b, offs, out):
                 x = work.tile([P, PIECE], F32, name="x", tag="x")
                 nc.vector.tensor_tensor(x[:], shifts[k][:].indirect(lists[i]), products[i][:], ADD)
                 x_rounded = work.tile([P, PIECE], BF16, name="x_rounded", tag="x_rounded")
-                nc.scalar.copy(x_rounded[:], x[:])
-                nc.tensor.matmul(
-                    totals[i][:], weights[:, k, :], x_rounded[:], start=(k == 0), stop=(k == n_blocks - 1)
-                )
+                if i < n_pieces - 1:
+                    nc.scalar.copy(x_rounded[:], x[:])
+                else:
+                    nc.vector.tensor_copy(x_rounded[:], x[:])
+                for h in range(2):
+                    nc.tensor.matmul(
+                        totals[2 * i + h][:],
+                        weights[:, k, :],
+                        x_rounded[:, h * HALF : (h + 1) * HALF],
+                        start=(k == 0),
+                        stop=(k == n_blocks - 1),
+                    )
 
-        for i in range(n_pieces):
-            result = work.tile([M, PIECE], F32, name="result", tag="result")
-            nc.scalar.activation(result[:], totals[i][:], RELU, bias=bias[:, 0:1])
-            nc.sync.dma_start(out[:, i * PIECE : (i + 1) * PIECE], result[:])
+        for q in range(2 * n_pieces):
+            result = work.tile([M, HALF], F32, name="result", tag="result")
+            columns = slice(q * HALF, (q + 1) * HALF)
+            if q < 2 * n_pieces - 1:
+                nc.scalar.activation(result[:], totals[q][:], RELU, bias=bias[:, 0:1])
+            else:
+                nc.vector.tensor_scalar(result[:], totals[q][:], bias[:, 0:1], 0.0, ADD, MAX)
+            nc.sync.dma_start(out[:, columns], result[:])

@@ -42,9 +42,9 @@ def tile_lookup_resglu_relu_kernel(tc, tab, y, w, b, offs, out):
             shifts.append(shift)
 
         weights = held.tile([P, n_blocks, M], BF16, name="weights")
-        nc.scalar.dma_start(weights[:], w.rearrange("(k p) m -> p k m", p=P))
+        nc.sync.dma_start(weights[:], w.rearrange("(k p) m -> p k m", p=P))
         bias = held.tile([M, 1], F32, name="bias")
-        nc.scalar.dma_start(bias[:], b)
+        nc.sync.dma_start(bias[:], b)
 
         totals = [sums.tile([M, HALF], F32, name=f"total{q}") for q in range(2 * n_pieces)]
         for k in range(n_blocks):
@@ -65,13 +65,14 @@ def tile_lookup_resglu_relu_kernel(tc, tab, y, w, b, offs, out):
                 x_rounded = work.tile([P, PIECE], BF16, name="x_rounded", tag="x_rounded")
                 if i < n_pieces - 1:
                     nc.scalar.copy(x_rounded[:], x[:])
-                else:
-                    nc.vector.tensor_copy(x_rounded[:], x[:])
                 for h in range(2):
+                    half = slice(h * HALF, (h + 1) * HALF)
+                    if i == n_pieces - 1:
+                        nc.vector.tensor_copy(x_rounded[:, half], x[:, half])
                     nc.tensor.matmul(
                         totals[2 * i + h][:],
                         weights[:, k, :],
-                        x_rounded[:, h * HALF : (h + 1) * HALF],
+                        x_rounded[:, half],
                         start=(k == 0),
                         stop=(k == n_blocks - 1),
                     )

import concourse.mybir as mybir

F32, BF16, U16 = mybir.dt.float32, mybir.dt.bfloat16, mybir.dt.uint16
MULT, ADD, MAX = mybir.AluOpType.mult, mybir.AluOpType.add, mybir.AluOpType.max
SILU, RELU = mybir.ActivationFunctionType.Silu, mybir.ActivationFunctionType.Relu

P = 128
ROWS = 256
PLACES = 2048
N = 1024
M = 128
PIECE = 512
HALF = PIECE // 2

FLOPS = 2 * ROWS * N * M


def tile_lookup_resglu_relu_kernel(tc, tab, y, w, b, offs, out):
    nc = tc.nc
    n_blocks = ROWS // P
    n_pieces = N // PIECE
    list_columns = PIECE // 16

    with (
        tc.tile_pool(name="held", bufs=1) as held,
        tc.tile_pool(name="work", bufs=n_blocks * n_pieces) as work,
        tc.psum_pool(name="sums", bufs=1) as sums,
    ):
        offsets = held.tile([P, N // 16], U16, name="offsets")
        nc.sync.dma_start(offsets[:], offs)
        gates, shifts, streams = [], [], []
        for k in range(n_blocks):
            rows = slice(k * P, (k + 1) * P)
            gate = held.tile([P, PLACES], F32, name=f"gate{k}")
            nc.sync.dma_start(gate[:], tab[0, rows, :])
            stream = held.tile([P, N], F32, name=f"stream{k}")
            nc.sync.dma_start(stream[:], y[rows, :])
            shift = held.tile([P, PLACES], F32, name=f"shift{k}")
            nc.sync.dma_start(shift[:], tab[1, rows, :])
            gates.append(gate)
            streams.append(stream)
            shifts.append(shift)

        weights = held.tile([P, n_blocks, M], BF16, name="weights")
        nc.sync.dma_start(weights[:], w.rearrange("(k p) m -> p k m", p=P))
        bias = held.tile([M, 1], F32, name="bias")
        nc.sync.dma_start(bias[:], b)

        totals = [sums.tile([M, HALF], F32, name=f"total{q}") for q in range(2 * n_pieces)]
        for k in range(n_blocks):
            lists = [offsets[:, i * list_columns : (i + 1) * list_columns] for i in range(n_pieces)]
            gated = []
            for i in range(n_pieces):
                part = work.tile([P, PIECE], F32, name="part", tag="part")
                nc.scalar.activation(part[:], gates[k][:].indirect(lists[i]), SILU)
                gated.append(part)
            products = []
            for i in range(n_pieces):
                product = work.tile([P, PIECE], F32, name="product", tag="product")
                nc.vector.tensor_tensor(product[:], gated[i][:], streams[k][:, i * PIECE : (i + 1) * PIECE], MULT)
                products.append(product)
            for i in range(n_pieces):
                x = work.tile([P, PIECE], F32, name="x", tag="x")
                nc.vector.tensor_tensor(x[:], shifts[k][:].indirect(lists[i]), products[i][:], ADD)
                x_rounded = work.tile([P, PIECE], BF16, name="x_rounded", tag="x_rounded")
                if i < n_pieces - 1:
                    nc.scalar.copy(x_rounded[:], x[:])
                for h in range(2):
                    half = slice(h * HALF, (h + 1) * HALF)
                    if i == n_pieces - 1:
                        nc.vector.tensor_copy(x_rounded[:, half], x[:, half])
                    nc.tensor.matmul(
                        totals[2 * i + h][:],
                        weights[:, k, :],
                        x_rounded[:, half],
                        start=(k == 0),
                        stop=(k == n_blocks - 1),
                    )

        for q in range(2 * n_pieces):
            result = work.tile([M, HALF], F32, name="result", tag="result")
            columns = slice(q * HALF, (q + 1) * HALF)
            if q < 2 * n_pieces - 1:
                nc.scalar.activation(result[:], totals[q][:], RELU, bias=bias[:, 0:1])
            else:
                nc.vector.tensor_scalar(result[:], totals[q][:], bias[:, 0:1], 0.0, ADD, MAX)
            nc.sync.dma_start(out[:, columns], result[:])
